import numpy as np
import ml_dtypes


def mxq(x, axis, fmt="e4m3"):
    dtype, down = {"e4m3": (ml_dtypes.float8_e4m3fn, 7), "e5m2": (ml_dtypes.float8_e5m2, 14)}[fmt]
    v = np.moveaxis(np.asarray(x, np.float32).astype(ml_dtypes.bfloat16).astype(np.float64), axis, -1)
    blocks = v.reshape(v.shape[:-1] + (-1, 32))
    amax = np.abs(blocks).max(-1, keepdims=True)
    byte = np.maximum(np.where(amax > 0, np.frexp(amax)[1] - 1 + 127, 0) - down, 1)
    scale = np.exp2(byte - 127.0)
    codes = (blocks / scale).astype(np.float32).astype(dtype).astype(np.float64)
    return np.moveaxis((codes * scale).reshape(v.shape), -1, axis)


WIDE = False


def mx_kscale(k):
    if not WIDE:
        return np.ones(k)
    levels = np.array([10, -10, 5, -5, 0])
    if k % 512:
        return np.exp2(np.random.permutation(np.resize(levels, k // 32))).repeat(32)
    a = np.empty((k // 512, 16))
    for p in range(k // 512):
        a[p, :8] = np.random.permutation(np.resize(levels, 8))
        for g in range(8):
            far = levels[np.abs(levels - a[p, g]) >= 10]
            a[p, g + 8] = far[np.random.randint(len(far))]
    return np.exp2(a.ravel()).repeat(32)


BF16 = ml_dtypes.bfloat16


def bf(x):
    return np.asarray(x, np.float32).astype(BF16)


def f64(x):
    return np.asarray(x).astype(np.float64)

def planes(Y):
    n, m = Y.shape
    b = f64(bf(Y)).reshape(n // 32, 32, m)
    amax = np.abs(b).max(1)
    byte = np.clip(np.where(amax > 0, np.frexp(amax)[1] - 1 + 127 - 7, 1), 1, 254)
    codes = (b * np.exp2(127.0 - byte)[:, None, :]).reshape(n, m).astype(np.float32).astype(ml_dtypes.float8_e4m3fn).view(np.uint8)
    words = codes.reshape(n // 512, 128, 4, m).transpose(0, 1, 3, 2)
    return np.ascontiguousarray(words), np.ascontiguousarray(byte.astype(np.uint8).reshape(n // 512, 16, m))


H, N, K, P, W = 4, 256, 512, 128, 16
K2 = 2 * K
T = P * W


def softplus(x):
    return np.maximum(x, 0.0) + np.log(1.0 + np.exp(-np.abs(x)))


def softmax_last(s):
    e = np.exp(s - np.max(s, axis=-1, keepdims=True))
    return e / np.sum(e, axis=-1, keepdims=True)


def setup_inputs():
    s = mx_kscale(K)
    r = mx_kscale(K2)
    t = mx_kscale(T)
    return {
        "q": bf(np.random.standard_normal((H, N, K)) * 1.5 * s),
        "k": bf(np.random.standard_normal((H, T, K)) / s),
        "v": bf(np.random.standard_normal((H, T, K)) / t[:, None]),
        "kb": bf(np.random.standard_normal((H, P, K2)) / r),
        "g": bf(np.random.standard_normal(K2) * r / np.concatenate([s, s])),
        "gt": bf(np.random.standard_normal(T) * 4.0 * t),
    }


def core(q, k, v, kb, g, gt):
    q, k, v, kb, g, gt = f64(q), f64(k), f64(v), f64(kb), f64(g), f64(gt)
    h, n, c = q.shape
    p = kb.shape[1]
    t = k.shape[1]
    scale = np.sqrt(c)

    f = np.concatenate([np.maximum(q, 0.0), np.minimum(q, 0.0)], axis=-1)
    f = f * g

    u = (mxq(f, 2, "e4m3") @ mxq(kb, 2, "e4m3").transpose(0, 2, 1)) / scale
    lg = -softplus(-u)

    s = (mxq(q, 2, "e4m3") @ mxq(k, 2, "e4m3").transpose(0, 2, 1)) / scale
    s = s.reshape(h, n, p, W) + lg[..., None]
    s = s.reshape(h, n, t)

    pr = softmax_last(s)
    a = pr * gt

    return mxq(a, 2, "e4m3") @ mxq(v, 1, "e4m3")


def reference(q, k, v, kb, g, gt):
    R_out = core(q, k, v, kb, g, gt)
    words, scales = planes(np.moveaxis(R_out, 2, 0).reshape(512, -1))
    return R_out, words, scales

@@ -1,0 +1,488 @@
+from contextlib import ExitStack
+import math
+
+import concourse.mybir as mybir
+from concourse.masks import make_identity
+
+F32 = mybir.dt.float32
+BF16 = mybir.dt.bfloat16
+U32 = mybir.dt.uint32
+I32 = mybir.dt.int32
+U8 = mybir.dt.uint8
+FP8X4 = mybir.dt.float8_e4m3fn_x4
+ACT = mybir.ActivationFunctionType
+ALU = mybir.AluOpType
+AX = mybir.AxisListType
+
+H, N, K, PAGES, W = 4, 256, 512, 128, 16
+K2 = 2 * K
+T = PAGES * W
+P = 128
+GROUPS = T // 512
+NT = N // P
+TILES = H * NT
+SCALE = 1.0 / math.sqrt(float(K))
+ROOT = math.sqrt(float(K))
+FLOPS = 2 * H * N * (K2 * PAGES + 2 * K * T)
+
+SB_BUFS = {
+    "ident": 1, "gtn": 1, "gtb": 1, "g8": 1, "gg": 1,
+    "qr": 4, "kbr": 4, "qT": 2, "kbT": 1, "pn": 1, "fT": 1,
+    "qc": 4, "qs": 4, "fc": 2, "fs": 2, "kbc": 2, "kbs": 2,
+    "kr": 5, "kT": 3, "kc": 8, "ks": 8,
+    "vr": 5, "vT": 3, "vc": 10, "vs": 10,
+    "s": 2, "e": 2, "a": 2, "aT": 2, "ac": 2, "asc": 2,
+    "lg": 1, "ax": 1, "rm": 3, "nm": 3, "rs": 3, "ri": 3,
+    "o": 2, "ob": 2, "obT": 2, "wq": 1, "wsc": 1,
+}
+PS_BUFS = {"tp": 3, "ps": 4, "po": 1}
+
+
+def tile_signsplitpagegateattention_kernel(tc, q, k, v, kb, g, gt, out_0, out_1, out_2):
+    nc = tc.nc
+    with ExitStack() as ctx:
+        pool = ctx.enter_context(tc.tile_pool(name="sb", bufs=1))
+        psum = ctx.enter_context(tc.psum_pool(name="pp", bufs=1))
+
+        def sb(tag, shape, dt):
+            return pool.tile(shape, dt, name=tag, tag=tag, bufs=SB_BUFS[tag], align_bytes=64)
+
+        def pt(tag):
+            return psum.tile([P, 512], F32, name=tag, tag=tag, bufs=PS_BUFS[tag])
+
+        ident = sb("ident", [P, P], F32)
+        make_identity(nc, ident[:])
+        g8 = sb("g8", [P, 2, 4], BF16)
+        gg = sb("gg", [P, 2, N, 4], BF16)
+        gtb = sb("gtb", [P, T], BF16)
+        lg = sb("lg", [P, TILES, PAGES], F32)
+        wq = sb("wq", [P, TILES * P], U32)
+        wsc = sb("wsc", [P, TILES * P], U8)
+
+        st = {}
+
+        def load_q(h):
+            t = sb("qr", [P, NT, K], BF16)
+            nc.sync.dma_start(out=t[:], in_=q[h].rearrange("(t p) k -> p t k", p=P))
+            st["qr", h] = t
+            t = sb("kbr", [P, K2], BF16)
+            nc.sync.dma_start(out=t[:], in_=kb[h])
+            st["kbr", h] = t
+
+        def load_kv(name, src, n):
+            t = sb(name, [P, 4, K], BF16)
+            h, gi = divmod(n, GROUPS)
+            nc.sync.dma_start(out=t[:], in_=src[h, gi * 512:(gi + 1) * 512, :].rearrange("(p j) k -> p j k", j=4))
+            st[name, n] = t
+
+        def load_k(n):
+            if n < H * GROUPS:
+                load_kv("kr", k, n)
+
+        def load_v(n):
+            if n < H * GROUPS:
+                load_kv("vr", v, n)
+
+        def transpose_words(src, starts, step, tag="tp"):
+            ps = pt(tag)
+            for x, s0 in enumerate(starts):
+                nc.tensor.transpose(ps[:, x * P:(x + 1) * P], src[:, s0:s0 + step * (P - 1) + 1:step], ident[:])
+            return ps
+
+        def q_tr(h):
+            w = st["qr", h][:].rearrange("p t k -> p (t k)").bitcast(F32)
+            st["qps", h] = transpose_words(w, [0, 1, 256, 257], 2, "tp")
+            w = st["kbr", h][:].bitcast(F32)
+            st["kbps", h] = transpose_words(w, [0, 1, 256, 257], 2, "tp")
+
+        def q_copy(h):
+            for src, dst in (("qps", "qT"), ("kbps", "kbT")):
+                t = sb(dst, [P, 1024], BF16)
+                nc.scalar.copy(
+                    out=t[:].bitcast(F32).rearrange("p (a r u) -> p a r u", a=2, u=2),
+                    in_=st[src, h][:].rearrange("p (a u r) -> p a r u", a=2, u=2))
+                st[dst, h] = t
+
+        def quant(src, cname, sname, words):
+            c = sb(cname, [P, words], U32)
+            s = sb(sname, [P, words], U8)
+            nc.vector.quantize_mx(out=c[:].bitcast(FP8X4), scales=s[:], in_=src)
+            return c, s
+
+        def q_quant(h):
+            st["q", h] = quant(st["qT", h][:], "qc", "qs", N)
+
+        def kb_quant(h):
+            st["kb", h] = quant(st["kbT", h][:], "kbc", "kbs", N)
+
+        def f_split(h):
+            pn = sb("pn", [P, 2, 4 * N], BF16)
+            nc.vector.tensor_scalar(out=pn[:, 0, :], in0=st["qT", h][:], scalar1=0.0, scalar2=None, op0=ALU.max)
+            nc.vector.tensor_scalar(out=pn[:, 1, :], in0=st["qT", h][:], scalar1=0.0, scalar2=None, op0=ALU.min)
+            st["pn", h] = pn
+
+        def f_gain(h):
+            f = sb("fT", [P, 8 * N], BF16)
+            nc.vector.tensor_tensor(
+                out=f[:], in0=st["pn", h][:].rearrange("p a x -> p (a x)"),
+                in1=gg[:].rearrange("p a n j -> p (a n j)"), op=ALU.mult)
+            st["fT", h] = f
+
+        def f_quant(h):
+            st["f", h] = quant(st["fT", h][:], "fc", "fs", 2 * N)
+
+        def u_mm(h):
+            hp, lo = divmod(h, 2)
+            if lo == 0:
+                st["u", hp] = pt("ps")
+            ps = st["u", hp]
+            fc, fs = st["f", h]
+            kc, ks = st["kb", h]
+            for t in range(NT):
+                c0 = (lo * NT + t) * PAGES
+                for x in range(2):
+                    fcol = slice(x * N + t * P, x * N + (t + 1) * P)
+                    kcol = slice(x * PAGES, (x + 1) * PAGES)
+                    nc.tensor.matmul_mx(
+                        out=ps[:, c0:c0 + PAGES],
+                        lhsT=fc[:, fcol].bitcast(FP8X4), lhsT_scale=fs[:, fcol],
+                        rhs=kc[:, kcol].bitcast(FP8X4), rhs_scale=ks[:, kcol],
+                        start=(x == 0), stop=(x == 1))
+
+        def k_tr(n, u):
+            w = st["kr", n][:].rearrange("p s k -> p (s k)").bitcast(F32)
+            st["kps", n, u] = transpose_words(w, [(2 * u + e) * 256 + x for e in range(2) for x in range(2)], 2)
+
+        def copy(eng, out, in_):
+            if eng == "v":
+                nc.vector.tensor_copy(out=out, in_=in_)
+            else:
+                nc.scalar.copy(out=out, in_=in_)
+
+        def k_copy(n, u, eng="s"):
+            if u == 0:
+                st["kT", n] = sb("kT", [P, 2048], BF16)
+            copy(
+                eng, out=st["kT", n][:].bitcast(F32)[:, u * 512:(u + 1) * 512].rearrange("p (r j) -> p r j", j=4),
+                in_=st["kps", n, u][:].rearrange("p (j r) -> p r j", j=4))
+
+        def k_quant(n):
+            st["k", n] = quant(st["kT", n][:], "kc", "ks", 512)
+
+        def v_inter(n, eng):
+            t = sb("vT", [P, 2048], BF16)
+            st["vT", n] = t
+            if eng == "g":
+                for x in range(2):
+                    nc.gpsimd.tensor_scalar(
+                        out=t[:, x * 1024:(x + 1) * 1024].rearrange("p (c j) -> p c j", j=4),
+                        in0=st["vr", n][:, :, x * 256:(x + 1) * 256].rearrange("p j c -> p c j"),
+                        scalar1=1.0, scalar2=0.0, op0=ALU.mult, op1=ALU.add)
+            else:
+                dst = t[:].rearrange("p (c i j) -> p c j i", i=4, j=4)
+                srcv = st["vr", n][:].rearrange("p j (c i) -> p c j i", i=4)
+                nc.scalar.copy(out=dst, in_=srcv)
+
+        def v_quant(n):
+            st["v", n] = quant(st["vT", n][:], "vc", "vs", 512)
+
+        def s_mm(i):
+            h, t = divmod(i, NT)
+            qc, qs = st["q", h]
+            col = slice(t * P, (t + 1) * P)
+            for c in range(GROUPS):
+                kc, ks = st["k", h * GROUPS + c]
+                ps = pt("ps")
+                nc.tensor.matmul_mx(
+                    out=ps[:], lhsT=qc[:, col].bitcast(FP8X4), lhsT_scale=qs[:, col],
+                    rhs=kc[:].bitcast(FP8X4), rhs_scale=ks[:], start=True, stop=True)
+                st["sps", i, c] = ps
+
+        def gate(i):
+            s = sb("s", [P, T], F32)
+            st["s", i] = s
+            for c in range(GROUPS):
+                row = lg[:, i, 32 * c:32 * (c + 1)].unsqueeze(1).unsqueeze(3).to_broadcast([P, 2, 32, 8])
+                nc.vector.tensor_tensor(
+                    out=s[:, c * 512:(c + 1) * 512].rearrange("p (u a b) -> p u a b", u=2, b=8),
+                    in0=st["sps", i, c][:].rearrange("p (u a b) -> p u a b", u=2, b=8),
+                    in1=row, op=ALU.add)
+
+        def row_max(i):
+            m = sb("rm", [P, 1], F32)
+            nc.vector.tensor_reduce(out=m[:], in_=st["s", i][:], axis=AX.X, op=ALU.max)
+            st["rm", i] = m
+
+        def exp_(i):
+            nm = sb("nm", [P, 1], F32)
+            nc.scalar.mul(nm[:], st["rm", i][:], -SCALE)
+            e = sb("e", [P, T], F32)
+            rs = sb("rs", [P, 1], F32)
+            nc.scalar.activation(out=e[:], in_=st["s", i][:], func=ACT.Exp, bias=nm[:], scale=SCALE, accum_out=rs[:])
+            st["e", i] = e
+            st["rs", i] = rs
+
+        def recip(i):
+            ri = sb("ri", [P, 1], F32)
+            nc.vector.reciprocal(out=ri[:], in_=st["rs", i][:])
+            st["ri", i] = ri
+
+        def weigh_gs(i, c1):
+            st["a", i] = sb("a", [P, T], BF16)
+            e = st["e", i]
+            nc.gpsimd.tensor_tensor(out=e[:, 0:c1], in0=e[:, 0:c1], in1=gtb[:, 0:c1], op=ALU.mult)
+
+        def weigh_s(i, c1):
+            nc.scalar.activation(out=st["a", i][:, 0:c1], in_=st["e", i][:, 0:c1], func=ACT.Copy, scale=st["ri", i][:])
+
+        def weigh_v(i, c0, c1):
+            nc.vector.scalar_tensor_tensor(
+                out=st["a", i][:, c0:c1], in0=st["e", i][:, c0:c1], scalar=st["ri", i][:], in1=gtb[:, c0:c1],
+                op0=ALU.mult, op1=ALU.mult)
+
+        def weigh(i, half):
+            if half == 0:
+                st["a", i] = sb("a", [P, T], BF16)
+            col = slice(half * 1024, (half + 1) * 1024)
+            nc.vector.scalar_tensor_tensor(
+                out=st["a", i][:, col], in0=st["e", i][:, col], scalar=st["ri", i][:], in1=gtb[:, col],
+                op0=ALU.mult, op1=ALU.mult)
+
+        def a_tr(i, half):
+            w = st["a", i][:].bitcast(F32)
+            st["aps", i, half] = transpose_words(w, [half * 512 + x * P for x in range(4)], 1)
+
+        def a_copy(i, half):
+            if half == 0:
+                st["aT", i] = sb("aT", [P, 2048], BF16)
+            nc.scalar.copy(
+                out=st["aT", i][:].bitcast(F32)[:, half * 512:(half + 1) * 512].rearrange("p (g n u) -> p g n u", g=2, u=2),
+                in_=st["aps", i, half][:].rearrange("p (g u n) -> p g n u", g=2, u=2))
+
+        def a_quant(i):
+            st["aq", i] = quant(st["aT", i][:], "ac", "asc", 512)
+
+        def pv_mm(i):
+            h = i // NT
+            ac, asc = st["aq", i]
+            ps = pt("po")
+            for c in range(GROUPS):
+                vc, vs = st["v", h * GROUPS + c]
+                col = slice(c * P, (c + 1) * P)
+                nc.tensor.matmul_mx(
+                    out=ps[:], lhsT=ac[:, col].bitcast(FP8X4), lhsT_scale=asc[:, col],
+                    rhs=vc[:].bitcast(FP8X4), rhs_scale=vs[:], start=(c == 0), stop=(c == GROUPS - 1))
+            st["ops", i] = ps
+
+        def o_copy(i):
+            h, t = divmod(i, NT)
+            o = sb("o", [P, K], F32)
+            nc.scalar.copy(out=o[:], in_=st["ops", i][:])
+            st["o", i] = o
+            nc.sync.dma_start(out=out_0[h, t * P:(t + 1) * P, :], in_=o[:])
+
+        def o_round(i):
+            ob = sb("ob", [P, K], BF16)
+            nc.vector.tensor_copy(out=ob[:], in_=st["o", i][:])
+            st["ob", i] = ob
+
+        def o_tr(i):
+            ps = pt("tp")
+            w = st["ob", i][:].bitcast(F32)
+            for x in range(2):
+                nc.tensor.transpose(ps[:, x * P:(x + 1) * P], w[:, x:x + 255:2], ident[:])
+            st["obps", i] = ps
+
+        def o_inter(i):
+            t = sb("obT", [P, 512], BF16)
+            nc.scalar.copy(
+                out=t[:].bitcast(F32).rearrange("p (n u) -> p n u", u=2),
+                in_=st["obps", i][:, 0:256].rearrange("p (u n) -> p n u", u=2))
+            st["obT", i] = t
+
+        def o_quant(i):
+            col = slice(i * P, (i + 1) * P)
+            nc.vector.quantize_mx(out=wq[:, col].bitcast(FP8X4), scales=wsc[:, col], in_=st["obT", i][:])
+            words = out_1[0].rearrange("p m t -> p (m t)").bitcast(I32)
+            nc.sync.dma_start(out=words[:, col], in_=wq[:, col].bitcast(I32))
+
+        def store_scales(c0, c1):
+            rows = out_2[0].bitcast(I32)
+            live = wsc[:].bitcast(I32)
+            for quad in range(4):
+                nc.sync.dma_start(
+                    out=rows[4 * quad:4 * quad + 4, c0 // 4:c1 // 4],
+                    in_=live[32 * quad:32 * quad + 4, c0 // 4:c1 // 4])
+
+        warm = sb("nm", [P, 1], F32)
+        nc.vector.memset(warm[:], 0.0)
+        nc.scalar.activation(out=warm[:], in_=warm[:], func=ACT.Exp)
+        nc.scalar.dma_start(out=g8[:], in_=g.rearrange("(x p j) -> p x j", x=2, j=4))
+        load_q(0)
+        load_q(1)
+        for n in range(4):
+            load_k(n)
+        load_q(2)
+        load_v(0)
+        load_q(3)
+        load_v(1)
+        gtn = sb("gtn", [P, T], BF16)
+        nc.sync.dma_start(out=gtn[:], in_=gt.partition_broadcast(P))
+        load_k(4)
+        for n in range(2, 5):
+            load_v(n)
+
+        nc.vector.tensor_copy(out=gg[:], in_=g8[:].unsqueeze(2).to_broadcast([P, 2, N, 4]))
+
+        def lg_scalar(hp):
+            ax = sb("ax", [P, 512], F32)
+            nc.scalar.activation(out=ax[:], in_=st["u", hp][:], func=ACT.Abs, scale=SCALE)
+            nc.scalar.activation(out=ax[:], in_=ax[:], func=ACT.Exp, scale=-1.0)
+            nc.scalar.activation(out=ax[:], in_=ax[:], func=ACT.Ln, bias=1.0)
+            st["ax", hp] = ax
+            warm = sb("nm", [P, 1], F32)
+            nc.scalar.activation(out=warm[:], in_=ax[:, 0:1], func=ACT.Exp)
+
+        def lg_root(hp):
+            ax = st["ax", hp]
+            nc.vector.tensor_scalar(out=ax[:], in0=ax[:], scalar1=ROOT, scalar2=None, op0=ALU.mult)
+
+        def lg_vector(hp):
+            nc.vector.scalar_tensor_tensor(
+                out=lg[:, 4 * hp:4 * hp + 4, :].rearrange("p i x -> p (i x)"), in0=st["u", hp][:], scalar=0.0,
+                in1=st["ax", hp][:], op0=ALU.min, op1=ALU.subtract)
+
+        def q_in(h):
+            q_tr(h)
+            q_copy(h)
+
+        def k_in(n):
+            for x in range(2):
+                k_tr(n, x)
+                k_copy(n, x)
+            load_k(n + 5)
+
+        q_in(0)
+        q_in(1)
+        for h in range(2):
+            f_split(h)
+            q_quant(h)
+            f_gain(h)
+            k_in(2 * h)
+            kb_quant(h)
+            f_quant(h)
+            u_mm(h)
+            k_in(2 * h + 1)
+            k_quant(2 * h)
+        q_in(2)
+        lg_scalar(0)
+        v_inter(0, "g")
+        k_quant(1)
+        k_quant(3)
+        s_mm(0)
+        f_split(2)
+        q_quant(2)
+        f_gain(2)
+        kb_quant(2)
+        lg_root(0)
+        f_quant(2)
+        lg_vector(0)
+        gate(0)
+        k_in(4)
+        k_in(5)
+        v_inter(1, "g")
+        v_inter(2, "s")
+
+        for i in range(TILES):
+            kn = [n for n in (6 + 2 * i, 7 + 2 * i) if n < H * GROUPS]
+            vn = [n for n in (4 + 2 * i, 5 + 2 * i) if n < H * GROUPS]
+            row_max(i)
+            if i >= 1:
+                a_tr(i - 1, 0)
+                a_copy(i - 1, 0)
+                a_tr(i - 1, 1)
+                a_copy(i - 1, 1)
+            if kn and i >= 1:
+                k_in(kn[0])
+            if i >= 1:
+                a_quant(i - 1)
+            if i + 1 < TILES:
+                s_mm(i + 1)
+            if i == 0:
+                v_inter(3, "g")
+                q_in(3)
+                k_quant(4)
+                k_quant(5)
+            exp_(i)
+            if i == 2:
+                lg_scalar(1)
+            if i >= 1 and vn:
+                v_inter(vn[1], "g")
+                load_v(vn[1] + 5)
+            if i == 0:
+                nc.vector.tensor_copy(
+                    out=gtb[:].bitcast(F32).rearrange("p (g u r) -> p g u r", g=4, u=2),
+                    in_=gtn[:].bitcast(F32).rearrange("p (g r u) -> p g u r", g=4, u=2))
+            if i + 1 < TILES:
+                gate(i + 1)
+            if i == 1:
+                u_mm(2)
+                u_mm(3)
+            if i == 0:
+                for n in range(4):
+                    v_quant(n)
+                    load_v(n + 5)
+                v_inter(vn[1], "g")
+                load_v(vn[1] + 5)
+                f_split(3)
+                q_quant(3)
+                f_gain(3)
+                k_in(kn[0])
+                kb_quant(3)
+                f_quant(3)
+            if i >= 1:
+                pv_mm(i - 1)
+                o_copy(i - 1)
+            if kn:
+                k_quant(kn[0])
+                k_in(kn[1])
+            if vn:
+                v_quant(vn[1])
+            if i == 2:
+                lg_root(1)
+            if i < 6 and i >= 1:
+                o_round(i - 1)
+                o_tr(i - 1)
+                o_inter(i - 1)
+            if i == 2:
+                lg_vector(1)
+            recip(i)
+            if i >= 6:
+                o_round(i - 1)
+                o_tr(i - 1)
+                o_inter(i - 1)
+            weigh(i, 0)
+            weigh(i, 1)
+            if kn:
+                k_quant(kn[1])
+            if i >= 1:
+                o_quant(i - 1)
+            if vn:
+                v_inter(vn[0], "s")
+                load_v(vn[0] + 5)
+                v_quant(vn[0])
+            if i == 5:
+                store_scales(0, 4 * P)
+        i = TILES - 1
+        a_tr(i, 0)
+        a_copy(i, 0)
+        a_tr(i, 1)
+        a_copy(i, 1)
+        a_quant(i)
+        pv_mm(i)
+        o_copy(i)
+        o_round(i)
+        o_tr(i)
+        o_inter(i)
+        o_quant(i)
+        store_scales(4 * P, 8 * P)

@@ -30,9 +30,9 @@ SB_BUFS = {
     "qr": 4, "kbr": 4, "qT": 2, "kbT": 1, "pn": 1, "fT": 1,
     "qc": 4, "qs": 4, "fc": 2, "fs": 2, "kbc": 2, "kbs": 2,
     "kr": 5, "kT": 3, "kc": 8, "ks": 8,
-    "vr": 5, "vT": 3, "vc": 10, "vs": 10,
+    "vr": 5, "vTs": 2, "vTg": 1, "vc": 8, "vs": 8,
     "s": 2, "e": 2, "a": 2, "aT": 2, "ac": 2, "asc": 2,
-    "lg": 1, "ax": 1, "rm": 3, "nm": 3, "rs": 3, "ri": 3,
+    "lg": 1, "rm": 3, "nm": 3, "rs": 3, "ri": 3,
     "o": 2, "ob": 2, "obT": 2, "wq": 1, "wsc": 1,
 }
 PS_BUFS = {"tp": 3, "ps": 4, "po": 1}
@@ -43,6 +43,7 @@ def tile_signsplitpagegateattention_kernel(tc, q, k, v, kb, g, gt, out_0, out_1,
     with ExitStack() as ctx:
         pool = ctx.enter_context(tc.tile_pool(name="sb", bufs=1))
         psum = ctx.enter_context(tc.psum_pool(name="pp", bufs=1))
+        ctx.enter_context(tc.manual_schedule())
 
         def sb(tag, shape, dt):
             return pool.tile(shape, dt, name=tag, tag=tag, bufs=SB_BUFS[tag], align_bytes=64)
@@ -170,7 +171,7 @@ def tile_signsplitpagegateattention_kernel(tc, q, k, v, kb, g, gt, out_0, out_1,
             st["k", n] = quant(st["kT", n][:], "kc", "ks", 512)
 
         def v_inter(n, eng):
-            t = sb("vT", [P, 2048], BF16)
+            t = sb("vT" + eng, [P, 2048], BF16)
             st["vT", n] = t
             if eng == "g":
                 for x in range(2):
@@ -236,43 +237,43 @@ def tile_signsplitpagegateattention_kernel(tc, q, k, v, kb, g, gt, out_0, out_1,
             nc.scalar.activation(out=st["a", i][:, 0:c1], in_=st["e", i][:, 0:c1], func=ACT.Copy, scale=st["ri", i][:])
 
         def weigh_v(i, c0, c1):
+            if c0 == 0:
+                st["a", i] = sb("a", [P, T], BF16)
             nc.vector.scalar_tensor_tensor(
                 out=st["a", i][:, c0:c1], in0=st["e", i][:, c0:c1], scalar=st["ri", i][:], in1=gtb[:, c0:c1],
                 op0=ALU.mult, op1=ALU.mult)
 
-        def weigh(i, half):
-            if half == 0:
-                st["a", i] = sb("a", [P, T], BF16)
-            col = slice(half * 1024, (half + 1) * 1024)
-            nc.vector.scalar_tensor_tensor(
-                out=st["a", i][:, col], in0=st["e", i][:, col], scalar=st["ri", i][:], in1=gtb[:, col],
-                op0=ALU.mult, op1=ALU.mult)
-
-        def a_tr(i, half):
+        def a_tr(i, g0, g1):
             w = st["a", i][:].bitcast(F32)
-            st["aps", i, half] = transpose_words(w, [half * 512 + x * P for x in range(4)], 1)
+            st["aps", i, g0] = transpose_words(w, [x * P for x in range(2 * g0, 2 * g1)], 1)
 
-        def a_copy(i, half):
-            if half == 0:
+        def a_copy(i, g0, g1, eng="s"):
+            if g0 == 0:
                 st["aT", i] = sb("aT", [P, 2048], BF16)
-            nc.scalar.copy(
-                out=st["aT", i][:].bitcast(F32)[:, half * 512:(half + 1) * 512].rearrange("p (g n u) -> p g n u", g=2, u=2),
-                in_=st["aps", i, half][:].rearrange("p (g u n) -> p g n u", g=2, u=2))
+            ng = g1 - g0
+            copy(
+                eng, out=st["aT", i][:].bitcast(F32)[:, g0 * 256:g1 * 256].rearrange("p (g n u) -> p g n u", g=ng, u=2),
+                in_=st["aps", i, g0][:, 0:256 * ng].rearrange("p (g u n) -> p g n u", g=ng, u=2))
 
-        def a_quant(i):
-            st["aq", i] = quant(st["aT", i][:], "ac", "asc", 512)
+        def a_quant(i, g0, g1):
+            if g0 == 0:
+                st["aq", i] = (sb("ac", [P, 512], U32), sb("asc", [P, 512], U8))
+            c, s = st["aq", i]
+            nc.vector.quantize_mx(
+                out=c[:, g0 * P:g1 * P].bitcast(FP8X4), scales=s[:, g0 * P:g1 * P],
+                in_=st["aT", i][:, g0 * 512:g1 * 512])
 
-        def pv_mm(i):
+        def pv_mm(i, g0, g1):
             h = i // NT
             ac, asc = st["aq", i]
-            ps = pt("po")
-            for c in range(GROUPS):
+            if g0 == 0:
+                st["ops", i] = pt("po")
+            for c in range(g0, g1):
                 vc, vs = st["v", h * GROUPS + c]
                 col = slice(c * P, (c + 1) * P)
                 nc.tensor.matmul_mx(
-                    out=ps[:], lhsT=ac[:, col].bitcast(FP8X4), lhsT_scale=asc[:, col],
+                    out=st["ops", i][:], lhsT=ac[:, col].bitcast(FP8X4), lhsT_scale=asc[:, col],
                     rhs=vc[:].bitcast(FP8X4), rhs_scale=vs[:], start=(c == 0), stop=(c == GROUPS - 1))
-            st["ops", i] = ps
 
         def o_copy(i):
             h, t = divmod(i, NT)
@@ -318,39 +319,24 @@ def tile_signsplitpagegateattention_kernel(tc, q, k, v, kb, g, gt, out_0, out_1,
         nc.vector.memset(warm[:], 0.0)
         nc.scalar.activation(out=warm[:], in_=warm[:], func=ACT.Exp)
         nc.scalar.dma_start(out=g8[:], in_=g.rearrange("(x p j) -> p x j", x=2, j=4))
-        load_q(0)
-        load_q(1)
-        for n in range(4):
+        for h in range(H):
+            load_q(h)
+        for n in range(5):
             load_k(n)
-        load_q(2)
-        load_v(0)
-        load_q(3)
-        load_v(1)
+        for n in range(2):
+            load_v(n)
         gtn = sb("gtn", [P, T], BF16)
         nc.sync.dma_start(out=gtn[:], in_=gt.partition_broadcast(P))
-        load_k(4)
         for n in range(2, 5):
             load_v(n)
 
         nc.vector.tensor_copy(out=gg[:], in_=g8[:].unsqueeze(2).to_broadcast([P, 2, N, 4]))
+        ax = sb("e", [P, T], F32)
 
-        def lg_scalar(hp):
-            ax = sb("ax", [P, 512], F32)
-            nc.scalar.activation(out=ax[:], in_=st["u", hp][:], func=ACT.Abs, scale=SCALE)
-            nc.scalar.activation(out=ax[:], in_=ax[:], func=ACT.Exp, scale=-1.0)
-            nc.scalar.activation(out=ax[:], in_=ax[:], func=ACT.Ln, bias=1.0)
-            st["ax", hp] = ax
-            warm = sb("nm", [P, 1], F32)
-            nc.scalar.activation(out=warm[:], in_=ax[:, 0:1], func=ACT.Exp)
-
-        def lg_root(hp):
-            ax = st["ax", hp]
-            nc.vector.tensor_scalar(out=ax[:], in0=ax[:], scalar1=ROOT, scalar2=None, op0=ALU.mult)
-
-        def lg_vector(hp):
-            nc.vector.scalar_tensor_tensor(
-                out=lg[:, 4 * hp:4 * hp + 4, :].rearrange("p i x -> p (i x)"), in0=st["u", hp][:], scalar=0.0,
-                in1=st["ax", hp][:], op0=ALU.min, op1=ALU.subtract)
+        def ax_exp(hp):
+            col = slice(hp * 512, (hp + 1) * 512)
+            nc.scalar.activation(out=ax[:, col], in_=st["u", hp][:], func=ACT.Abs, scale=SCALE)
+            nc.scalar.activation(out=ax[:, col], in_=ax[:, col], func=ACT.Exp, scale=-1.0)
 
         def q_in(h):
             q_tr(h)
@@ -364,125 +350,124 @@ def tile_signsplitpagegateattention_kernel(tc, q, k, v, kb, g, gt, out_0, out_1,
 
         q_in(0)
         q_in(1)
-        for h in range(2):
+        for h in range(H):
             f_split(h)
             q_quant(h)
             f_gain(h)
-            k_in(2 * h)
+            if h < 2:
+                q_in(h + 2)
+            k_in(h)
             kb_quant(h)
             f_quant(h)
             u_mm(h)
-            k_in(2 * h + 1)
-            k_quant(2 * h)
-        q_in(2)
-        lg_scalar(0)
-        v_inter(0, "g")
-        k_quant(1)
-        k_quant(3)
-        s_mm(0)
-        f_split(2)
-        q_quant(2)
-        f_gain(2)
-        kb_quant(2)
-        lg_root(0)
-        f_quant(2)
-        lg_vector(0)
-        gate(0)
-        k_in(4)
-        k_in(5)
+            if h >= 1:
+                k_quant(h - 1)
+            if h == 2:
+                ax_exp(0)
+        ax_exp(1)
+        nc.scalar.activation(out=ax[:, 0:1024], in_=ax[:, 0:1024], func=ACT.Ln, bias=1.0)
         v_inter(1, "g")
+        warm = sb("nm", [P, 1], F32)
+        nc.scalar.activation(out=warm[:], in_=ax[:, 0:1], func=ACT.Exp)
+        k_quant(3)
+        for x in range(2):
+            k_tr(4, x)
+            k_copy(4, x, "v")
+        load_k(9)
+        v_inter(0, "s")
+        nc.vector.tensor_copy(
+            out=gtb[:].bitcast(F32).rearrange("p (g u r) -> p g u r", g=4, u=2),
+            in_=gtn[:].bitcast(F32).rearrange("p (g r u) -> p g u r", g=4, u=2))
+        k_quant(4)
+        s_mm(0)
+        nc.vector.tensor_scalar(out=ax[:, 0:1024], in0=ax[:, 0:1024], scalar1=ROOT, scalar2=None, op0=ALU.mult)
+        v_quant(1)
+        v_inter(3, "g")
+        k_in(5)
+        for hp in range(2):
+            nc.vector.scalar_tensor_tensor(
+                out=lg[:, 4 * hp:4 * hp + 4, :].rearrange("p i x -> p (i x)"), in0=st["u", hp][:], scalar=0.0,
+                in1=ax[:, hp * 512:(hp + 1) * 512], op0=ALU.min, op1=ALU.subtract)
         v_inter(2, "s")
+        gate(0)
+        s_mm(1)
+        k_quant(5)
+        v_quant(0)
+        for n in range(5, 9):
+            load_v(n)
 
         for i in range(TILES):
             kn = [n for n in (6 + 2 * i, 7 + 2 * i) if n < H * GROUPS]
-            vn = [n for n in (4 + 2 * i, 5 + 2 * i) if n < H * GROUPS]
+            vn = [n for n in (2 + 2 * i, 3 + 2 * i) if n < H * GROUPS]
+            vnext = [n for n in (4 + 2 * i, 5 + 2 * i) if n < H * GROUPS]
             row_max(i)
             if i >= 1:
-                a_tr(i - 1, 0)
-                a_copy(i - 1, 0)
-                a_tr(i - 1, 1)
-                a_copy(i - 1, 1)
-            if kn and i >= 1:
-                k_in(kn[0])
-            if i >= 1:
-                a_quant(i - 1)
-            if i + 1 < TILES:
-                s_mm(i + 1)
-            if i == 0:
-                v_inter(3, "g")
-                q_in(3)
-                k_quant(4)
-                k_quant(5)
-            exp_(i)
-            if i == 2:
-                lg_scalar(1)
-            if i >= 1 and vn:
-                v_inter(vn[1], "g")
-                load_v(vn[1] + 5)
-            if i == 0:
-                nc.vector.tensor_copy(
-                    out=gtb[:].bitcast(F32).rearrange("p (g u r) -> p g u r", g=4, u=2),
-                    in_=gtn[:].bitcast(F32).rearrange("p (g r u) -> p g u r", g=4, u=2))
+                a_tr(i - 1, 2, 4)
+                a_copy(i - 1, 2, 4)
+            if i >= 2:
+                o_tr(i - 2)
+            for x, n in enumerate(kn):
+                k_in(n)
+                if x == 0:
+                    if i >= 2:
+                        o_inter(i - 2)
+                    exp_(i)
+            if not kn:
+                if i >= 2:
+                    o_inter(i - 2)
+                exp_(i)
             if i + 1 < TILES:
                 gate(i + 1)
-            if i == 1:
-                u_mm(2)
-                u_mm(3)
-            if i == 0:
-                for n in range(4):
-                    v_quant(n)
-                    load_v(n + 5)
-                v_inter(vn[1], "g")
-                load_v(vn[1] + 5)
-                f_split(3)
-                q_quant(3)
-                f_gain(3)
-                k_in(kn[0])
-                kb_quant(3)
-                f_quant(3)
             if i >= 1:
-                pv_mm(i - 1)
-                o_copy(i - 1)
+                a_quant(i - 1, 0, 4)
+                pv_mm(i - 1, 0, 4)
             if kn:
                 k_quant(kn[0])
-                k_in(kn[1])
+            if i >= 2:
+                o_quant(i - 2)
             if vn:
-                v_quant(vn[1])
-            if i == 2:
-                lg_root(1)
-            if i < 6 and i >= 1:
-                o_round(i - 1)
-                o_tr(i - 1)
-                o_inter(i - 1)
-            if i == 2:
-                lg_vector(1)
-            recip(i)
-            if i >= 6:
-                o_round(i - 1)
-                o_tr(i - 1)
-                o_inter(i - 1)
-            weigh(i, 0)
-            weigh(i, 1)
+                v_quant(vn[0])
+            if vnext:
+                v_inter(vnext[0], "s")
+                load_v(vnext[0] + 5)
             if kn:
                 k_quant(kn[1])
+            if i + 2 < TILES:
+                s_mm(i + 2)
             if i >= 1:
-                o_quant(i - 1)
+                o_copy(i - 1)
+            recip(i)
+            if i + 1 < TILES:
+                weigh_v(i, 0, 1024)
+                a_tr(i, 0, 2)
+                a_copy(i, 0, 2)
+                weigh_v(i, 1024, 2048)
+            if i >= 1:
+                o_round(i - 1)
             if vn:
-                v_inter(vn[0], "s")
-                load_v(vn[0] + 5)
-                v_quant(vn[0])
-            if i == 5:
-                store_scales(0, 4 * P)
+                v_quant(vn[1])
+            if vnext:
+                v_inter(vnext[1], "g")
+                load_v(vnext[1] + 5)
+            if i == 6:
+                store_scales(0, 5 * P)
         i = TILES - 1
-        a_tr(i, 0)
-        a_copy(i, 0)
-        a_tr(i, 1)
-        a_copy(i, 1)
-        a_quant(i)
-        pv_mm(i)
+        o_tr(i - 1)
+        o_inter(i - 1)
+        for c in range(GROUPS):
+            weigh_v(i, c * 512, (c + 1) * 512)
+            if c >= 2:
+                a_quant(i, c - 2, c - 1)
+                pv_mm(i, c - 2, c - 1)
+            a_tr(i, c, c + 1)
+            a_copy(i, c, c + 1)
+        o_quant(i - 1)
+        for c in range(2, GROUPS):
+            a_quant(i, c, c + 1)
+            pv_mm(i, c, c + 1)
         o_copy(i)
         o_round(i)
         o_tr(i)
         o_inter(i)
         o_quant(i)
-        store_scales(4 * P, 8 * P)
+        store_scales(5 * P, 8 * P)

from contextlib import ExitStack
import math

import concourse.mybir as mybir
from concourse.masks import make_identity

F32 = mybir.dt.float32
BF16 = mybir.dt.bfloat16
U32 = mybir.dt.uint32
I32 = mybir.dt.int32
U8 = mybir.dt.uint8
FP8X4 = mybir.dt.float8_e4m3fn_x4
ACT = mybir.ActivationFunctionType
ALU = mybir.AluOpType
AX = mybir.AxisListType

H, N, K, PAGES, W = 4, 256, 512, 128, 16
K2 = 2 * K
T = PAGES * W
P = 128
GROUPS = T // 512
NT = N // P
TILES = H * NT
SCALE = 1.0 / math.sqrt(float(K))
ROOT = math.sqrt(float(K))
FLOPS = 2 * H * N * (K2 * PAGES + 2 * K * T)

SB_BUFS = {
    "ident": 1, "gtn": 1, "gtb": 1, "g8": 1, "gg": 1,
    "qr": 4, "kbr": 4, "qT": 2, "kbT": 1, "pn": 1, "fT": 1,
    "qc": 4, "qs": 4, "fc": 2, "fs": 2, "kbc": 2, "kbs": 2,
    "kr": 5, "kT": 3, "kc": 8, "ks": 8,
    "vr": 5, "vTs": 2, "vTg": 1, "vc": 8, "vs": 8,
    "s": 2, "e": 2, "a": 2, "aT": 2, "ac": 2, "asc": 2,
    "lg": 1, "rm": 3, "nm": 3, "rs": 3, "ri": 3,
    "o": 2, "ob": 2, "obT": 2, "wq": 1, "wsc": 1,
}
PS_BUFS = {"tp": 3, "ps": 4, "po": 1}


def tile_signsplitpagegateattention_kernel(tc, q, k, v, kb, g, gt, out_0, out_1, out_2):
    nc = tc.nc
    with ExitStack() as ctx:
        pool = ctx.enter_context(tc.tile_pool(name="sb", bufs=1))
        psum = ctx.enter_context(tc.psum_pool(name="pp", bufs=1))
        ctx.enter_context(tc.manual_schedule())

        def sb(tag, shape, dt):
            return pool.tile(shape, dt, name=tag, tag=tag, bufs=SB_BUFS[tag], align_bytes=64)

        def pt(tag):
            return psum.tile([P, 512], F32, name=tag, tag=tag, bufs=PS_BUFS[tag])

        ident = sb("ident", [P, P], F32)
        make_identity(nc, ident[:])
        g8 = sb("g8", [P, 2, 4], BF16)
        gg = sb("gg", [P, 2, N, 4], BF16)
        gtb = sb("gtb", [P, T], BF16)
        lg = sb("lg", [P, TILES, PAGES], F32)
        wq = sb("wq", [P, TILES * P], U32)
        wsc = sb("wsc", [P, TILES * P], U8)

        st = {}

        def load_q(h):
            t = sb("qr", [P, NT, K], BF16)
            nc.sync.dma_start(out=t[:], in_=q[h].rearrange("(t p) k -> p t k", p=P))
            st["qr", h] = t
            t = sb("kbr", [P, K2], BF16)
            nc.sync.dma_start(out=t[:], in_=kb[h])
            st["kbr", h] = t

        def load_kv(name, src, n):
            t = sb(name, [P, 4, K], BF16)
            h, gi = divmod(n, GROUPS)
            nc.sync.dma_start(out=t[:], in_=src[h, gi * 512:(gi + 1) * 512, :].rearrange("(p j) k -> p j k", j=4))
            st[name, n] = t

        def load_k(n):
            if n < H * GROUPS:
                load_kv("kr", k, n)

        def load_v(n):
            if n < H * GROUPS:
                load_kv("vr", v, n)

        def transpose_words(src, starts, step, tag="tp"):
            ps = pt(tag)
            for x, s0 in enumerate(starts):
                nc.tensor.transpose(ps[:, x * P:(x + 1) * P], src[:, s0:s0 + step * (P - 1) + 1:step], ident[:])
            return ps

        def q_tr(h):
            w = st["qr", h][:].rearrange("p t k -> p (t k)").bitcast(F32)
            st["qps", h] = transpose_words(w, [0, 1, 256, 257], 2, "tp")
            w = st["kbr", h][:].bitcast(F32)
            st["kbps", h] = transpose_words(w, [0, 1, 256, 257], 2, "tp")

        def q_copy(h):
            for src, dst in (("qps", "qT"), ("kbps", "kbT")):
                t = sb(dst, [P, 1024], BF16)
                nc.scalar.copy(
                    out=t[:].bitcast(F32).rearrange("p (a r u) -> p a r u", a=2, u=2),
                    in_=st[src, h][:].rearrange("p (a u r) -> p a r u", a=2, u=2))
                st[dst, h] = t

        def quant(src, cname, sname, words):
            c = sb(cname, [P, words], U32)
            s = sb(sname, [P, words], U8)
            nc.vector.quantize_mx(out=c[:].bitcast(FP8X4), scales=s[:], in_=src)
            return c, s

        def q_quant(h):
            st["q", h] = quant(st["qT", h][:], "qc", "qs", N)

        def kb_quant(h):
            st["kb", h] = quant(st["kbT", h][:], "kbc", "kbs", N)

        def f_split(h):
            pn = sb("pn", [P, 2, 4 * N], BF16)
            nc.vector.tensor_scalar(out=pn[:, 0, :], in0=st["qT", h][:], scalar1=0.0, scalar2=None, op0=ALU.max)
            nc.vector.tensor_scalar(out=pn[:, 1, :], in0=st["qT", h][:], scalar1=0.0, scalar2=None, op0=ALU.min)
            st["pn", h] = pn

        def f_gain(h):
            f = sb("fT", [P, 8 * N], BF16)
            nc.vector.tensor_tensor(
                out=f[:], in0=st["pn", h][:].rearrange("p a x -> p (a x)"),
                in1=gg[:].rearrange("p a n j -> p (a n j)"), op=ALU.mult)
            st["fT", h] = f

        def f_quant(h):
            st["f", h] = quant(st["fT", h][:], "fc", "fs", 2 * N)

        def u_mm(h):
            hp, lo = divmod(h, 2)
            if lo == 0:
                st["u", hp] = pt("ps")
            ps = st["u", hp]
            fc, fs = st["f", h]
            kc, ks = st["kb", h]
            for t in range(NT):
                c0 = (lo * NT + t) * PAGES
                for x in range(2):
                    fcol = slice(x * N + t * P, x * N + (t + 1) * P)
                    kcol = slice(x * PAGES, (x + 1) * PAGES)
                    nc.tensor.matmul_mx(
                        out=ps[:, c0:c0 + PAGES],
                        lhsT=fc[:, fcol].bitcast(FP8X4), lhsT_scale=fs[:, fcol],
                        rhs=kc[:, kcol].bitcast(FP8X4), rhs_scale=ks[:, kcol],
                        start=(x == 0), stop=(x == 1))

        def k_tr(n, u):
            w = st["kr", n][:].rearrange("p s k -> p (s k)").bitcast(F32)
            st["kps", n, u] = transpose_words(w, [(2 * u + e) * 256 + x for e in range(2) for x in range(2)], 2)

        def copy(eng, out, in_):
            if eng == "v":
                nc.vector.tensor_copy(out=out, in_=in_)
            else:
                nc.scalar.copy(out=out, in_=in_)

        def k_copy(n, u, eng="s"):
            if u == 0:
                st["kT", n] = sb("kT", [P, 2048], BF16)
            copy(
                eng, out=st["kT", n][:].bitcast(F32)[:, u * 512:(u + 1) * 512].rearrange("p (r j) -> p r j", j=4),
                in_=st["kps", n, u][:].rearrange("p (j r) -> p r j", j=4))

        def k_quant(n):
            st["k", n] = quant(st["kT", n][:], "kc", "ks", 512)

        def v_inter(n, eng):
            t = sb("vT" + eng, [P, 2048], BF16)
            st["vT", n] = t
            if eng == "g":
                for x in range(2):
                    nc.gpsimd.tensor_scalar(
                        out=t[:, x * 1024:(x + 1) * 1024].rearrange("p (c j) -> p c j", j=4),
                        in0=st["vr", n][:, :, x * 256:(x + 1) * 256].rearrange("p j c -> p c j"),
                        scalar1=1.0, scalar2=0.0, op0=ALU.mult, op1=ALU.add)
            else:
                dst = t[:].rearrange("p (c i j) -> p c j i", i=4, j=4)
                srcv = st["vr", n][:].rearrange("p j (c i) -> p c j i", i=4)
                nc.scalar.copy(out=dst, in_=srcv)

        def v_quant(n):
            st["v", n] = quant(st["vT", n][:], "vc", "vs", 512)

        def s_mm(i):
            h, t = divmod(i, NT)
            qc, qs = st["q", h]
            col = slice(t * P, (t + 1) * P)
            for c in range(GROUPS):
                kc, ks = st["k", h * GROUPS + c]
                ps = pt("ps")
                nc.tensor.matmul_mx(
                    out=ps[:], lhsT=qc[:, col].bitcast(FP8X4), lhsT_scale=qs[:, col],
                    rhs=kc[:].bitcast(FP8X4), rhs_scale=ks[:], start=True, stop=True)
                st["sps", i, c] = ps

        def gate(i):
            s = sb("s", [P, T], F32)
            st["s", i] = s
            for c in range(GROUPS):
                row = lg[:, i, 32 * c:32 * (c + 1)].unsqueeze(1).unsqueeze(3).to_broadcast([P, 2, 32, 8])
                nc.vector.tensor_tensor(
                    out=s[:, c * 512:(c + 1) * 512].rearrange("p (u a b) -> p u a b", u=2, b=8),
                    in0=st["sps", i, c][:].rearrange("p (u a b) -> p u a b", u=2, b=8),
                    in1=row, op=ALU.add)

        def row_max(i):
            m = sb("rm", [P, 1], F32)
            nc.vector.tensor_reduce(out=m[:], in_=st["s", i][:], axis=AX.X, op=ALU.max)
            st["rm", i] = m

        def exp_(i):
            nm = sb("nm", [P, 1], F32)
            nc.scalar.mul(nm[:], st["rm", i][:], -SCALE)
            e = sb("e", [P, T], F32)
            rs = sb("rs", [P, 1], F32)
            nc.scalar.activation(out=e[:], in_=st["s", i][:], func=ACT.Exp, bias=nm[:], scale=SCALE, accum_out=rs[:])
            st["e", i] = e
            st["rs", i] = rs

        def recip(i):
            ri = sb("ri", [P, 1], F32)
            nc.vector.reciprocal(out=ri[:], in_=st["rs", i][:])
            st["ri", i] = ri

        def weigh_gs(i, c1):
            st["a", i] = sb("a", [P, T], BF16)
            e = st["e", i]
            nc.gpsimd.tensor_tensor(out=e[:, 0:c1], in0=e[:, 0:c1], in1=gtb[:, 0:c1], op=ALU.mult)

        def weigh_s(i, c1):
            nc.scalar.activation(out=st["a", i][:, 0:c1], in_=st["e", i][:, 0:c1], func=ACT.Copy, scale=st["ri", i][:])

        def weigh_v(i, c0, c1):
            if c0 == 0:
                st["a", i] = sb("a", [P, T], BF16)
            nc.vector.scalar_tensor_tensor(
                out=st["a", i][:, c0:c1], in0=st["e", i][:, c0:c1], scalar=st["ri", i][:], in1=gtb[:, c0:c1],
                op0=ALU.mult, op1=ALU.mult)

        def a_tr(i, g0, g1):
            w = st["a", i][:].bitcast(F32)
            st["aps", i, g0] = transpose_words(w, [x * P for x in range(2 * g0, 2 * g1)], 1)

        def a_copy(i, g0, g1, eng="s"):
            if g0 == 0:
                st["aT", i] = sb("aT", [P, 2048], BF16)
            ng = g1 - g0
            copy(
                eng, out=st["aT", i][:].bitcast(F32)[:, g0 * 256:g1 * 256].rearrange("p (g n u) -> p g n u", g=ng, u=2),
                in_=st["aps", i, g0][:, 0:256 * ng].rearrange("p (g u n) -> p g n u", g=ng, u=2))

        def a_quant(i, g0, g1):
            if g0 == 0:
                st["aq", i] = (sb("ac", [P, 512], U32), sb("asc", [P, 512], U8))
            c, s = st["aq", i]
            nc.vector.quantize_mx(
                out=c[:, g0 * P:g1 * P].bitcast(FP8X4), scales=s[:, g0 * P:g1 * P],
                in_=st["aT", i][:, g0 * 512:g1 * 512])

        def pv_mm(i, g0, g1):
            h = i // NT
            ac, asc = st["aq", i]
            if g0 == 0:
                st["ops", i] = pt("po")
            for c in range(g0, g1):
                vc, vs = st["v", h * GROUPS + c]
                col = slice(c * P, (c + 1) * P)
                nc.tensor.matmul_mx(
                    out=st["ops", i][:], lhsT=ac[:, col].bitcast(FP8X4), lhsT_scale=asc[:, col],
                    rhs=vc[:].bitcast(FP8X4), rhs_scale=vs[:], start=(c == 0), stop=(c == GROUPS - 1))

        def o_copy(i):
            h, t = divmod(i, NT)
            o = sb("o", [P, K], F32)
            nc.scalar.copy(out=o[:], in_=st["ops", i][:])
            st["o", i] = o
            nc.sync.dma_start(out=out_0[h, t * P:(t + 1) * P, :], in_=o[:])

        def o_round(i):
            ob = sb("ob", [P, K], BF16)
            nc.vector.tensor_copy(out=ob[:], in_=st["o", i][:])
            st["ob", i] = ob

        def o_tr(i):
            ps = pt("tp")
            w = st["ob", i][:].bitcast(F32)
            for x in range(2):
                nc.tensor.transpose(ps[:, x * P:(x + 1) * P], w[:, x:x + 255:2], ident[:])
            st["obps", i] = ps

        def o_inter(i):
            t = sb("obT", [P, 512], BF16)
            nc.scalar.copy(
                out=t[:].bitcast(F32).rearrange("p (n u) -> p n u", u=2),
                in_=st["obps", i][:, 0:256].rearrange("p (u n) -> p n u", u=2))
            st["obT", i] = t

        def o_quant(i):
            col = slice(i * P, (i + 1) * P)
            nc.vector.quantize_mx(out=wq[:, col].bitcast(FP8X4), scales=wsc[:, col], in_=st["obT", i][:])
            words = out_1[0].rearrange("p m t -> p (m t)").bitcast(I32)
            nc.sync.dma_start(out=words[:, col], in_=wq[:, col].bitcast(I32))

        def store_scales(c0, c1):
            rows = out_2[0].bitcast(I32)
            live = wsc[:].bitcast(I32)
            for quad in range(4):
                nc.sync.dma_start(
                    out=rows[4 * quad:4 * quad + 4, c0 // 4:c1 // 4],
                    in_=live[32 * quad:32 * quad + 4, c0 // 4:c1 // 4])

        warm = sb("nm", [P, 1], F32)
        nc.vector.memset(warm[:], 0.0)
        nc.scalar.activation(out=warm[:], in_=warm[:], func=ACT.Exp)
        nc.scalar.dma_start(out=g8[:], in_=g.rearrange("(x p j) -> p x j", x=2, j=4))
        for h in range(H):
            load_q(h)
        for n in range(5):
            load_k(n)
        for n in range(2):
            load_v(n)
        gtn = sb("gtn", [P, T], BF16)
        nc.sync.dma_start(out=gtn[:], in_=gt.partition_broadcast(P))
        for n in range(2, 5):
            load_v(n)

        nc.vector.tensor_copy(out=gg[:], in_=g8[:].unsqueeze(2).to_broadcast([P, 2, N, 4]))
        ax = sb("e", [P, T], F32)

        def ax_exp(hp):
            col = slice(hp * 512, (hp + 1) * 512)
            nc.scalar.activation(out=ax[:, col], in_=st["u", hp][:], func=ACT.Abs, scale=SCALE)
            nc.scalar.activation(out=ax[:, col], in_=ax[:, col], func=ACT.Exp, scale=-1.0)

        def q_in(h):
            q_tr(h)
            q_copy(h)

        def k_in(n):
            for x in range(2):
                k_tr(n, x)
                k_copy(n, x)
            load_k(n + 5)

        q_in(0)
        q_in(1)
        for h in range(H):
            f_split(h)
            q_quant(h)
            f_gain(h)
            if h < 2:
                q_in(h + 2)
            k_in(h)
            kb_quant(h)
            f_quant(h)
            u_mm(h)
            if h >= 1:
                k_quant(h - 1)
            if h == 2:
                ax_exp(0)
        ax_exp(1)
        nc.scalar.activation(out=ax[:, 0:1024], in_=ax[:, 0:1024], func=ACT.Ln, bias=1.0)
        v_inter(1, "g")
        warm = sb("nm", [P, 1], F32)
        nc.scalar.activation(out=warm[:], in_=ax[:, 0:1], func=ACT.Exp)
        k_quant(3)
        for x in range(2):
            k_tr(4, x)
            k_copy(4, x, "v")
        load_k(9)
        v_inter(0, "s")
        nc.vector.tensor_copy(
            out=gtb[:].bitcast(F32).rearrange("p (g u r) -> p g u r", g=4, u=2),
            in_=gtn[:].bitcast(F32).rearrange("p (g r u) -> p g u r", g=4, u=2))
        k_quant(4)
        s_mm(0)
        nc.vector.tensor_scalar(out=ax[:, 0:1024], in0=ax[:, 0:1024], scalar1=ROOT, scalar2=None, op0=ALU.mult)
        v_quant(1)
        v_inter(3, "g")
        k_in(5)
        for hp in range(2):
            nc.vector.scalar_tensor_tensor(
                out=lg[:, 4 * hp:4 * hp + 4, :].rearrange("p i x -> p (i x)"), in0=st["u", hp][:], scalar=0.0,
                in1=ax[:, hp * 512:(hp + 1) * 512], op0=ALU.min, op1=ALU.subtract)
        v_inter(2, "s")
        gate(0)
        s_mm(1)
        k_quant(5)
        v_quant(0)
        for n in range(5, 9):
            load_v(n)

        for i in range(TILES):
            kn = [n for n in (6 + 2 * i, 7 + 2 * i) if n < H * GROUPS]
            vn = [n for n in (2 + 2 * i, 3 + 2 * i) if n < H * GROUPS]
            vnext = [n for n in (4 + 2 * i, 5 + 2 * i) if n < H * GROUPS]
            row_max(i)
            if i >= 1:
                a_tr(i - 1, 2, 4)
                a_copy(i - 1, 2, 4)
            if i >= 2:
                o_tr(i - 2)
            for x, n in enumerate(kn):
                k_in(n)
                if x == 0:
                    if i >= 2:
                        o_inter(i - 2)
                    exp_(i)
            if not kn:
                if i >= 2:
                    o_inter(i - 2)
                exp_(i)
            if i + 1 < TILES:
                gate(i + 1)
            if i >= 1:
                a_quant(i - 1, 0, 4)
                pv_mm(i - 1, 0, 4)
            if kn:
                k_quant(kn[0])
            if i >= 2:
                o_quant(i - 2)
            if vn:
                v_quant(vn[0])
            if vnext:
                v_inter(vnext[0], "s")
                load_v(vnext[0] + 5)
            if kn:
                k_quant(kn[1])
            if i + 2 < TILES:
                s_mm(i + 2)
            if i >= 1:
                o_copy(i - 1)
            recip(i)
            if i + 1 < TILES:
                weigh_v(i, 0, 1024)
                a_tr(i, 0, 2)
                a_copy(i, 0, 2)
                weigh_v(i, 1024, 2048)
            if i >= 1:
                o_round(i - 1)
            if vn:
                v_quant(vn[1])
            if vnext:
                v_inter(vnext[1], "g")
                load_v(vnext[1] + 5)
            if i == 6:
                store_scales(0, 5 * P)
        i = TILES - 1
        o_tr(i - 1)
        o_inter(i - 1)
        for c in range(GROUPS):
            weigh_v(i, c * 512, (c + 1) * 512)
            if c >= 2:
                a_quant(i, c - 2, c - 1)
                pv_mm(i, c - 2, c - 1)
            a_tr(i, c, c + 1)
            a_copy(i, c, c + 1)
        o_quant(i - 1)
        for c in range(2, GROUPS):
            a_quant(i, c, c + 1)
            pv_mm(i, c, c + 1)
        o_copy(i)
        o_round(i)
        o_tr(i)
        o_inter(i)
        o_quant(i)
        store_scales(5 * P, 8 * P)
